import numpy as np
import ml_dtypes


def mxq(x, axis, fmt="e4m3"):
    dtype, down = {"e4m3": (ml_dtypes.float8_e4m3fn, 7), "e5m2": (ml_dtypes.float8_e5m2, 14)}[fmt]
    v = np.moveaxis(np.asarray(x, np.float32).astype(ml_dtypes.bfloat16).astype(np.float64), axis, -1)
    blocks = v.reshape(v.shape[:-1] + (-1, 32))
    amax = np.abs(blocks).max(-1, keepdims=True)
    byte = np.maximum(np.where(amax > 0, np.frexp(amax)[1] - 1 + 127, 0) - down, 1)
    scale = np.exp2(byte - 127.0)
    codes = (blocks / scale).astype(np.float32).astype(dtype).astype(np.float64)
    return np.moveaxis((codes * scale).reshape(v.shape), -1, axis)


WIDE = False


def mx_kscale(k):
    if not WIDE:
        return np.ones(k)
    levels = np.array([30, -30])
    if k % 512:
        return np.exp2(np.random.permutation(np.resize(levels, k // 32))).repeat(32)
    a = np.empty((k // 512, 16))
    for p in range(k // 512):
        a[p, :8] = np.random.permutation(np.resize(levels, 8))
        for g in range(8):
            far = levels[np.abs(levels - a[p, g]) >= 10]
            a[p, g + 8] = far[np.random.randint(len(far))]
    return np.exp2(a.ravel()).repeat(32)


def f64(x):
    return np.asarray(x).astype(np.float64)


def striped(idx):
    return np.tile(np.asarray(idx).reshape(-1, 16).T, (8, 1)).astype(np.uint16)


def unstriped(offs):
    return offs[:16].T.reshape(-1).astype(np.int64)


E2M1 = np.array([0.0, 0.5, 1.0, 1.5, 2.0, 3.0, 4.0, 6.0, -0.0, -0.5, -1.0, -1.5, -2.0, -3.0, -4.0, -6.0])


def pack_weight(w, fmt):
    k, n = w.shape
    w = f64(np.asarray(w, np.float32).astype(ml_dtypes.bfloat16)).reshape(k // 32, 32, n)
    amax = np.abs(w).max(1)
    if fmt in ("e4m3", "e5m2"):
        byte = np.frexp(amax)[1] - 1 + 127 - (7 if fmt == "e4m3" else 14)
    else:
        mant, ex = np.frexp(amax / 6.0)
        byte = np.where(mant > 0.5, ex, ex - 1) + 127
    byte = np.clip(np.where(amax > 0, byte, 1), 1, 254)
    scaled = (w * np.exp2(127.0 - byte)[:, None, :]).reshape(k, n).astype(np.float32)
    by_word = np.ascontiguousarray(scaled.reshape(k // 512, 128, 4, n).transpose(0, 1, 3, 2))
    if fmt in ("e4m3", "e5m2"):
        words = by_word.astype(ml_dtypes.float8_e4m3fn if fmt == "e4m3" else ml_dtypes.float8_e5m2).view(np.uint8)
    else:
        c = by_word.astype(ml_dtypes.float4_e2m1fn).view(np.uint8) & 0xF
        words = (c[..., 0::2] | (c[..., 1::2] << 4)).reshape(k // 512, 128, 2 * n)
    return np.ascontiguousarray(words), np.ascontiguousarray(byte.astype(np.uint8).reshape(k // 512, 16, n))


def unpack_weight(words, scales, fmt):
    g, _, n = scales.shape
    words = np.ascontiguousarray(words).reshape(g, 128, n, -1)
    if fmt in ("e4m3", "e5m2"):
        vals = words.view(ml_dtypes.float8_e4m3fn if fmt == "e4m3" else ml_dtypes.float8_e5m2).astype(np.float64)
    else:
        nib = np.empty((g, 128, n, 4), np.uint8)
        nib[..., 0::2] = words & 0xF
        nib[..., 1::2] = words >> 4
        vals = E2M1[nib]
    vals = vals * np.repeat(np.exp2(scales.astype(np.float64) - 127.0), 8, axis=1)[..., None]
    return vals.transpose(0, 1, 3, 2).reshape(g * 512, n)


def bf(x):
    return np.asarray(x, np.float32).astype(ml_dtypes.bfloat16)


def planes(Y):
    r, m = Y.shape
    b = f64(bf(Y)).reshape(r // 32, 32, m)
    amax = np.abs(b).max(1)
    byte = np.clip(np.where(amax > 0, np.frexp(amax)[1] - 1 + 127 - 7, 1), 1, 254)
    codes = (b * np.exp2(127.0 - byte)[:, None, :]).reshape(r, m).astype(np.float32).astype(ml_dtypes.float8_e4m3fn).view(np.uint8)
    words = codes.reshape(r // 512, 128, 4, m).transpose(0, 1, 3, 2)
    return np.ascontiguousarray(words), np.ascontiguousarray(byte.astype(np.uint8).reshape(r // 512, 16, m))


K, T, J, R, N, Z = 1024, 1024, 256, 512, 512, 512


def setup_inputs():
    n = np.random.standard_normal
    idx = np.random.permutation(T)[:J]
    idx2 = np.random.permutation(T)[:J]
    idx3 = np.random.permutation(Z)[:J]
    fk = mx_kscale(K)
    fr = mx_kscale(R)
    wp = pack_weight(n((K, R)) * 1 / np.sqrt(K) * fk[:, None] * fr, "e5m2")
    wbp = pack_weight(n((R, N)) * 1 / np.sqrt(R) / fr[:, None], "e2m1")
    return {
        "xf": (n((K, T))).astype(np.float32),
        "fk": (np.random.uniform(0.5, 2.0, (K, 1)) / fk[:, None]).astype(np.float32),
        "w_words": wp[0],
        "w_scales": wp[1],
        "wb_words": wbp[0],
        "wb_scales": wbp[1],
        "tz": (n((N, Z)) * 0.6).astype(np.float32),
        "rw": (np.random.uniform(0.5, 2.0, (1, J))).astype(np.float32),
        "offs": striped(idx),
        "offs2": striped(idx2),
        "offs3": striped(idx3),
    }


def reference(xf, fk, w_words, w_scales, wb_words, wb_scales, tz, rw, offs, offs2, offs3):
    idx = unstriped(offs)
    idx2 = unstriped(offs2)
    idx3 = unstriped(offs3)
    wu = unpack_weight(w_words, w_scales, "e5m2")
    wbu = unpack_weight(wb_words, wb_scales, "e2m1")
    u = np.maximum(f64(xf)[:, idx], f64(xf)[:, idx2]) * f64(fk)
    uq = mxq(u, 0, "e5m2")
    a = wu.T @ uq
    hid = np.maximum(a, 0.0)
    hidq = mxq(hid, 0, "e5m2")
    p = wbu.T @ hidq
    y = np.maximum(p, f64(tz)[:, idx3]) * f64(rw)
    words, scales = planes(y)
    return y, words, scales

@@ -1,0 +1,289 @@
+from contextlib import ExitStack
+
+import concourse.mybir as mybir
+from concourse.masks import make_identity
+
+K, T, J, R, N, Z = 1024, 1024, 256, 512, 512, 512
+FLOPS = 2 * K * R * J + 2 * R * N * J
+
+F32 = mybir.dt.float32
+BF16 = mybir.dt.bfloat16
+I32 = mybir.dt.int32
+U32 = mybir.dt.uint32
+U16 = mybir.dt.uint16
+U8 = mybir.dt.uint8
+E5M2 = mybir.dt.float8_e5m2_x4
+E4M3 = mybir.dt.float8_e4m3fn_x4
+E2M1 = mybir.dt.float4_e2m1fn_x4
+MAX = mybir.AluOpType.max
+MULT = mybir.AluOpType.mult
+COPY = mybir.ActivationFunctionType.Copy
+RELU = mybir.ActivationFunctionType.Relu
+
+P = 128
+PACK = 4
+PASSES = K // (P * PACK)
+HALF = J // 2
+LIST_COLS = J // 16
+
+
+def tile_list_largerpicks_plain_floored_pl_kernel(
+    tc, xf, fk, w_words, w_scales, wb_words, wb_scales, tz, rw, offs, offs2, offs3, out_0, out_1, out_2
+):
+    nc = tc.nc
+    with ExitStack() as ctx:
+        keep = ctx.enter_context(tc.tile_pool(name="keep", bufs=1))
+        psum = ctx.enter_context(tc.psum_pool(name="psum", bufs=1))
+
+        def tile(name, shape, dtype, tag=""):
+            return keep.tile(shape, dtype, name=name, tag=tag or name, align_bytes=64)
+
+        list_a = tile("list_a", [P, LIST_COLS], U16)
+        list_b = tile("list_b", [P, LIST_COLS], U16)
+        list_z = tile("list_z", [P, LIST_COLS], U16)
+        x_planes = [tile("x%d" % i, [P, T], F32) for i in range(PASSES * PACK)]
+        tz_planes = [tile("tz%d" % t, [P, Z], F32) for t in range(PACK)]
+        fk_sb = tile("fk_sb", [P, PASSES, PACK], F32)
+        rw_col = tile("rw_col", [P, 2], F32)
+        ident = tile("ident", [P, P], F32)
+        w_raw = [tile("w_raw%d" % g, [P, R], U32) for g in range(PASSES)]
+        ws_raw = tile("ws_raw", [P, PASSES, R], U8)
+        ws_dealt = tile("ws_dealt", [P, PASSES, R], U8)
+        wb_raw = tile("wb_raw", [P, 2 * N], U8)
+        wbs_raw = tile("wbs_raw", [P, N], U8)
+        wbs_dealt = tile("wbs_dealt", [P, N], U8)
+
+        x_rows = xf.rearrange("(g p t) c -> g t p c", p=P, t=PACK)
+        tz_rows = tz.rearrange("(p t) z -> t p z", t=PACK)
+
+        nc.gpsimd.memset(ws_raw[:].rearrange("p g c -> p (g c)").bitcast(U32), 0)
+        nc.gpsimd.memset(wbs_raw[:].bitcast(U32), 0)
+        make_identity(nc, ident[:])
+
+        def load_x(i):
+            nc.sync.dma_start(out=x_planes[i][:], in_=x_rows[i // PACK, i % PACK])
+
+        def load_w_scales(q):
+            nc.sync.dma_start(
+                out=ws_raw[32 * q : 32 * q + 4, :, :].bitcast(I32),
+                in_=w_scales[:, 4 * q : 4 * q + 4, :].rearrange("g r c -> r g c").bitcast(I32),
+            )
+
+        def load_wb_scales(q):
+            nc.sync.dma_start(
+                out=wbs_raw[32 * q : 32 * q + 4, :].bitcast(I32),
+                in_=wb_scales[0, 4 * q : 4 * q + 4, :].bitcast(I32),
+            )
+
+        load_x(0)
+        nc.sync.dma_start(list_a[:], offs)
+        nc.sync.dma_start(list_b[:], offs2)
+        load_x(1)
+        nc.sync.dma_start(out=fk_sb[:], in_=fk.rearrange("(g p t) o -> p g (t o)", p=P, t=PACK))
+        load_x(2)
+        load_w_scales(0)
+        load_w_scales(1)
+        load_x(3)
+        load_w_scales(2)
+        load_w_scales(3)
+        load_x(4)
+        load_wb_scales(0)
+        load_wb_scales(1)
+        load_x(5)
+        load_wb_scales(2)
+        load_wb_scales(3)
+        load_x(6)
+        nc.sync.dma_start(out=rw_col[:], in_=rw.rearrange("o (p e) -> p (o e)", e=2))
+        nc.sync.dma_start(list_z[:], offs3)
+        load_x(7)
+        for g in range(PASSES):
+            nc.sync.dma_start(
+                out=w_raw[g][:].bitcast(I32), in_=w_words[g].rearrange("p c r -> p (c r)").bitcast(I32)
+            )
+        for t in range(PACK):
+            if t == 2:
+                nc.sync.dma_start(out=wb_raw[:].bitcast(I32), in_=wb_words[0].bitcast(I32))
+            nc.sync.dma_start(out=tz_planes[t][:], in_=tz_rows[t])
+
+        def gather(on_vector, out, window, offsets):
+            if on_vector:
+                nc.vector.tensor_copy(out, window.indirect(offsets))
+            else:
+                nc.scalar.activation(out, window.indirect(offsets), COPY)
+
+        def deal(out, in_, run):
+            nc.vector.tensor_copy(
+                out=out.rearrange("p (t c i) -> p c t i", t=PACK, i=run),
+                in_=in_.rearrange("p (c i t) -> p c t i", t=PACK, i=run),
+            )
+
+        def half_cols(h):
+            return slice(h * HALF, (h + 1) * HALF)
+
+        def half_list(h):
+            return slice(h * LIST_COLS // 2, (h + 1) * LIST_COLS // 2)
+
+        def scale_and_round(out, larger, g):
+            n = out.shape[1]
+            nc.vector.tensor_tensor(
+                out=out,
+                in0=larger.rearrange("p t j -> p j t"),
+                in1=fk_sb[:, g, :].unsqueeze(1).to_broadcast([P, n, PACK]),
+                op=MULT,
+            )
+
+        def quantize(codes, scales, grouped, fmt):
+            nc.vector.quantize_mx(
+                out=codes.bitcast(fmt), scales=scales, in_=grouped.rearrange("p j t -> p (j t)")
+            )
+
+        larger = [tile("larger%d" % g, [P, PACK, J], F32) for g in range(PASSES)]
+        vector_gathers = (0, 1, 2, 6)
+        last = PASSES * PACK - 1
+
+        def plane_max(i):
+            pick_a = tile("pick_a%d" % i, [P, J], F32)
+            pick_b = tile("pick_b%d" % i, [P, J], F32)
+            gather(i in vector_gathers, pick_a[:], x_planes[i][:], list_a[:])
+            gather(False, pick_b[:], x_planes[i][:], list_b[:])
+            nc.vector.tensor_tensor(out=larger[i // PACK][:, i % PACK, :], in0=pick_a[:], in1=pick_b[:], op=MAX)
+
+        for i in range(PACK - 1):
+            plane_max(i)
+        for g in range(PASSES):
+            deal(ws_dealt[:, g, :], ws_raw[:, g, :], 16)
+        plane_max(PACK - 1)
+        u0 = tile("u0", [P, J, PACK], BF16)
+        u0_codes = tile("u0_codes", [P, J], U32)
+        u0_scales = tile("u0_scales", [P, J], U8)
+        scale_and_round(u0[:], larger[0][:], 0)
+        plane_max(4)
+        quantize(u0_codes[:], u0_scales[:], u0[:], E5M2)
+        deal(wbs_dealt[:], wbs_raw[:], 16)
+        plane_max(5)
+        plane_max(6)
+
+        rw_all = psum.tile([P, 2, P], F32, name="rw_all")
+        for e in range(2):
+            nc.tensor.transpose(rw_all[:, e, :], rw_col[:, e : e + 1].to_broadcast([P, P]), ident[:])
+
+        pick_a = [tile("last_a%d" % h, [P, HALF], F32) for h in range(2)]
+        pick_b = [tile("last_b%d" % h, [P, HALF], F32) for h in range(2)]
+        gather(True, pick_a[0][:], x_planes[last][:], list_a[:, half_list(0)])
+        gather(False, pick_b[0][:], x_planes[last][:], list_b[:, half_list(0)])
+        gather(False, pick_a[1][:], x_planes[last][:], list_a[:, half_list(1)])
+        gather(False, pick_b[1][:], x_planes[last][:], list_b[:, half_list(1)])
+
+        u1 = [tile("u1_%d" % h, [P, HALF, PACK], BF16) for h in range(2)]
+        u1_codes = [tile("u1_codes%d" % h, [P, HALF], U32) for h in range(2)]
+        u1_scales = [tile("u1_scales%d" % h, [P, HALF], U8) for h in range(2)]
+
+        def last_max(h):
+            nc.vector.tensor_tensor(
+                out=larger[1][:, PACK - 1, half_cols(h)], in0=pick_a[h][:], in1=pick_b[h][:], op=MAX
+            )
+
+        last_max(0)
+        w_dealt = [tile("w_dealt0", [P, R], U32, tag="last_a0")]
+        deal(w_dealt[0][:], w_raw[0][:], 4)
+        scale_and_round(u1[0][:], larger[1][:, :, half_cols(0)], 1)
+        w_dealt.append(tile("w_dealt1", [P, R], U32, tag="w_raw0"))
+        deal(w_dealt[1][:], w_raw[1][:], 4)
+        quantize(u1_codes[0][:], u1_scales[0][:], u1[0][:], E5M2)
+        last_max(1)
+        scale_and_round(u1[1][:], larger[1][:, :, half_cols(1)], 1)
+        quantize(u1_codes[1][:], u1_scales[1][:], u1[1][:], E5M2)
+        wb_dealt = tile("wb_dealt", [P, 2 * N], U8, tag="u1_1")
+        deal(wb_dealt[:].bitcast(U16), wb_raw[:].bitcast(U16), 8)
+
+        a_bank = [psum.tile([P, PACK, HALF], F32, name="a_bank%d" % h) for h in range(2)]
+
+        def first_product(h, g, codes, scales):
+            for t in range(PACK):
+                nc.tensor.matmul_mx(
+                    out=a_bank[h][:, t, :],
+                    lhsT=w_dealt[g][:, t * P : (t + 1) * P].bitcast(E5M2),
+                    lhsT_scale=ws_dealt[:, g, t * P : (t + 1) * P],
+                    rhs=codes.bitcast(E5M2),
+                    rhs_scale=scales,
+                    start=(g == 0 and t == 0),
+                    stop=(g == PASSES - 1 and t == PACK - 1),
+                )
+
+        first_product(0, 0, u0_codes[:, half_cols(0)], u0_scales[:, half_cols(0)])
+        first_product(1, 0, u0_codes[:, half_cols(1)], u0_scales[:, half_cols(1)])
+        first_product(0, 1, u1_codes[0][:], u1_scales[0][:])
+        first_product(1, 1, u1_codes[1][:], u1_scales[1][:])
+
+        def gather_floor(on_vector, h):
+            high = tile("floor_high%d" % h, [P, 2, HALF], F32, tag="hid%d" % h)
+            for t in range(2):
+                gather(on_vector, high[:, t, :], tz_planes[2 + t][:], list_z[:, half_list(h)])
+            return high
+
+        hid = [tile("hid%d" % h, [P, HALF, PACK], BF16) for h in range(2)]
+        hid_codes = [tile("hid_codes%d" % h, [P, HALF], U32) for h in range(2)]
+        hid_scales = [tile("hid_scales%d" % h, [P, HALF], U8) for h in range(2)]
+        p_bank = [psum.tile([P, PACK, HALF], F32, name="p_bank%d" % h) for h in range(2)]
+
+        def second_product(h):
+            nc.scalar.activation(hid[h][:], a_bank[h][:].rearrange("p t j -> p j t"), RELU)
+            quantize(hid_codes[h][:], hid_scales[h][:], hid[h][:], E5M2)
+            for t in range(PACK):
+                nc.tensor.matmul_mx(
+                    out=p_bank[h][:, t, :],
+                    lhsT=wb_dealt[:, 2 * t * P : 2 * (t + 1) * P].bitcast(E2M1),
+                    lhsT_scale=wbs_dealt[:, t * P : (t + 1) * P],
+                    rhs=hid_codes[h][:].bitcast(E5M2),
+                    rhs_scale=hid_scales[h][:],
+                    start=True,
+                    stop=True,
+                )
+
+        floor_low = tile("floor_low", [P, 2, J], F32, tag="x%d" % last)
+        for t in range(2):
+            gather(False, floor_low[:, t, :], tz_planes[t][:], list_z[:])
+        second_product(0)
+        floor_high = [gather_floor(True, 0)]
+        second_product(1)
+        floor_high.append(gather_floor(False, 1))
+
+        y_rows = out_0.rearrange("(p t) j -> p t j", t=PACK)
+        y_words = out_1[0].rearrange("p c r -> p (c r)")
+        y_scales = tile("y_scales", [P, J], U8)
+        floored = [tile("floored%d" % h, [P, PACK, HALF], F32) for h in range(2)]
+        y = [tile("y%d" % h, [P, PACK, HALF], F32) for h in range(2)]
+        y_grouped = [tile("y_grouped%d" % h, [P, HALF, PACK], BF16) for h in range(2)]
+        y_codes = [tile("y_codes%d" % h, [P, HALF], U32) for h in range(2)]
+
+        def finish(h):
+            low = floor_low[:, :, half_cols(h)]
+            high = floor_high[h][:]
+            nc.vector.tensor_tensor(out=floored[h][:, 0:2, :], in0=p_bank[h][:, 0:2, :], in1=low, op=MAX)
+            nc.vector.tensor_tensor(out=floored[h][:, 2:4, :], in0=p_bank[h][:, 2:4, :], in1=high, op=MAX)
+            weights = rw_all[:, :, h * (P // 2) : (h + 1) * (P // 2)].rearrange("p e q -> p q e")
+            nc.vector.tensor_tensor(
+                out=y[h][:].rearrange("p t (q e) -> p t q e", e=2),
+                in0=floored[h][:].rearrange("p t (q e) -> p t q e", e=2),
+                in1=weights.unsqueeze(1).to_broadcast([P, PACK, P // 2, 2]),
+                op=MULT,
+            )
+            nc.sync.dma_start(out=y_rows[:, :, half_cols(h)], in_=y[h][:])
+
+        def planes(h):
+            quantize(y_codes[h][:], y_scales[:, half_cols(h)], y_grouped[h][:], E4M3)
+            nc.sync.dma_start(
+                out=y_words[:, PACK * h * HALF : PACK * (h + 1) * HALF].bitcast(I32), in_=y_codes[h][:].bitcast(I32)
+            )
+
+        finish(0)
+        nc.scalar.copy(out=y_grouped[0][:], in_=y[0][:].rearrange("p t j -> p j t"))
+        finish(1)
+        planes(0)
+        nc.vector.tensor_copy(out=y_grouped[1][:], in_=y[1][:].rearrange("p t j -> p j t"))
+        planes(1)
+        for q in range(4):
+            queue = nc.sync if q % 2 == 0 else nc.scalar
+            queue.dma_start(
+                out=out_2[0, 4 * q : 4 * q + 4, :].bitcast(I32), in_=y_scales[32 * q : 32 * q + 4, :].bitcast(I32)
+            )

@@ -51,17 +51,24 @@ def tile_list_largerpicks_plain_floored_pl_kernel(
         ws_dealt = tile("ws_dealt", [P, PASSES, R], U8)
         wb_raw = tile("wb_raw", [P, 2 * N], U8)
         wbs_raw = tile("wbs_raw", [P, N], U8)
-        wbs_dealt = tile("wbs_dealt", [P, N], U8)
 
         x_rows = xf.rearrange("(g p t) c -> g t p c", p=P, t=PACK)
         tz_rows = tz.rearrange("(p t) z -> t p z", t=PACK)
 
+        zero_col = tile("zero_col", [P, 1], F32)
+        nc.vector.memset(zero_col[:], 0.0)
+        nc.scalar.activation(ident[:], zero_col[:].to_broadcast([P, P]), COPY)
         nc.gpsimd.memset(ws_raw[:].rearrange("p g c -> p (g c)").bitcast(U32), 0)
         nc.gpsimd.memset(wbs_raw[:].bitcast(U32), 0)
-        make_identity(nc, ident[:])
+        make_identity(nc, ident[:], nomemset=True)
 
         def load_x(i):
             nc.sync.dma_start(out=x_planes[i][:], in_=x_rows[i // PACK, i % PACK])
+
+        def load_w(g):
+            nc.sync.dma_start(
+                out=w_raw[g][:].bitcast(I32), in_=w_words[g].rearrange("p c r -> p (c r)").bitcast(I32)
+            )
 
         def load_w_scales(q):
             nc.sync.dma_start(
@@ -70,11 +77,13 @@ def tile_list_largerpicks_plain_floored_pl_kernel(
             )
 
         def load_wb_scales(q):
-            nc.sync.dma_start(
+            nc.gpsimd.dma_start(
                 out=wbs_raw[32 * q : 32 * q + 4, :].bitcast(I32),
                 in_=wb_scales[0, 4 * q : 4 * q + 4, :].bitcast(I32),
             )
 
+        for q in range(4):
+            load_wb_scales(q)
         load_x(0)
         nc.sync.dma_start(list_a[:], offs)
         nc.sync.dma_start(list_b[:], offs2)
@@ -87,22 +96,16 @@ def tile_list_largerpicks_plain_floored_pl_kernel(
         load_w_scales(2)
         load_w_scales(3)
         load_x(4)
-        load_wb_scales(0)
-        load_wb_scales(1)
         load_x(5)
-        load_wb_scales(2)
-        load_wb_scales(3)
+        with nc.allow_non_contiguous_dma(reason="one weight to a partition"):
+            nc.sync.dma_start(out=rw_col[:], in_=rw.rearrange("o (h p) -> p (o h)", p=P))
+        load_w(0)
         load_x(6)
-        nc.sync.dma_start(out=rw_col[:], in_=rw.rearrange("o (p e) -> p (o e)", e=2))
-        nc.sync.dma_start(list_z[:], offs3)
         load_x(7)
-        for g in range(PASSES):
-            nc.sync.dma_start(
-                out=w_raw[g][:].bitcast(I32), in_=w_words[g].rearrange("p c r -> p (c r)").bitcast(I32)
-            )
+        load_w(1)
+        nc.sync.dma_start(out=wb_raw[:].bitcast(I32), in_=wb_words[0].bitcast(I32))
+        nc.sync.dma_start(list_z[:], offs3)
         for t in range(PACK):
-            if t == 2:
-                nc.sync.dma_start(out=wb_raw[:].bitcast(I32), in_=wb_words[0].bitcast(I32))
             nc.sync.dma_start(out=tz_planes[t][:], in_=tz_rows[t])
 
         def gather(on_vector, out, window, offsets):
@@ -123,13 +126,10 @@ def tile_list_largerpicks_plain_floored_pl_kernel(
         def half_list(h):
             return slice(h * LIST_COLS // 2, (h + 1) * LIST_COLS // 2)
 
-        def scale_and_round(out, larger, g):
-            n = out.shape[1]
-            nc.vector.tensor_tensor(
-                out=out,
-                in0=larger.rearrange("p t j -> p j t"),
-                in1=fk_sb[:, g, :].unsqueeze(1).to_broadcast([P, n, PACK]),
-                op=MULT,
+        def interleave(copy, out, in_):
+            copy(
+                out=out.rearrange("p (c i) t -> p c t i", i=4),
+                in_=in_.rearrange("p t (c i) -> p c t i", i=4),
             )
 
         def quantize(codes, scales, grouped, fmt):
@@ -137,38 +137,58 @@ def tile_list_largerpicks_plain_floored_pl_kernel(
                 out=codes.bitcast(fmt), scales=scales, in_=grouped.rearrange("p j t -> p (j t)")
             )
 
-        larger = [tile("larger%d" % g, [P, PACK, J], F32) for g in range(PASSES)]
-        vector_gathers = (0, 1, 2, 6)
+        u_planes = tile("u_planes", [P, PACK, J], BF16)
+        larger0 = tile("larger0", [P, PACK, J], F32)
+        vector_gathers = (0, 1, 2)
         last = PASSES * PACK - 1
 
-        def plane_max(i):
+        def scale(on_vector, out, larger, i):
+            factor = fk_sb[:, i // PACK, i % PACK : i % PACK + 1]
+            if on_vector:
+                nc.vector.tensor_scalar(out, larger, factor, None, MULT)
+            else:
+                nc.scalar.activation(out, larger, COPY, scale=factor)
+
+        def plane(i):
             pick_a = tile("pick_a%d" % i, [P, J], F32)
             pick_b = tile("pick_b%d" % i, [P, J], F32)
+            larger = larger0[:, i, :] if i < PACK else tile("larger%d" % i, [P, J], F32)[:]
             gather(i in vector_gathers, pick_a[:], x_planes[i][:], list_a[:])
             gather(False, pick_b[:], x_planes[i][:], list_b[:])
-            nc.vector.tensor_tensor(out=larger[i // PACK][:, i % PACK, :], in0=pick_a[:], in1=pick_b[:], op=MAX)
+            nc.vector.tensor_tensor(out=larger, in0=pick_a[:], in1=pick_b[:], op=MAX)
+            if i >= PACK:
+                scale(True, u_planes[:, i % PACK, :], larger, i)
 
-        for i in range(PACK - 1):
-            plane_max(i)
-        for g in range(PASSES):
-            deal(ws_dealt[:, g, :], ws_raw[:, g, :], 16)
-        plane_max(PACK - 1)
         u0 = tile("u0", [P, J, PACK], BF16)
         u0_codes = tile("u0_codes", [P, J], U32)
         u0_scales = tile("u0_scales", [P, J], U8)
-        scale_and_round(u0[:], larger[0][:], 0)
-        plane_max(4)
+        for i in range(PACK - 1):
+            plane(i)
+        for g in range(PASSES):
+            deal(ws_dealt[:, g, :], ws_raw[:, g, :], 16)
+        plane(PACK - 1)
+        nc.vector.tensor_tensor(
+            out=u0[:],
+            in0=larger0[:].rearrange("p t j -> p j t"),
+            in1=fk_sb[:, 0:1, :].to_broadcast([P, J, PACK]),
+            op=MULT,
+        )
+        plane(PACK)
         quantize(u0_codes[:], u0_scales[:], u0[:], E5M2)
+        w_dealt = [tile("w_dealt0", [P, R], U32, tag="pick_a%d" % PACK)]
+        deal(w_dealt[0][:], w_raw[0][:], 4)
+        plane(PACK + 1)
+        wbs_dealt = tile("wbs_dealt", [P, N], U8, tag="pick_a%d" % (PACK + 1))
         deal(wbs_dealt[:], wbs_raw[:], 16)
-        plane_max(5)
-        plane_max(6)
+        plane(PACK + 2)
 
-        rw_all = psum.tile([P, 2, P], F32, name="rw_all")
-        for e in range(2):
-            nc.tensor.transpose(rw_all[:, e, :], rw_col[:, e : e + 1].to_broadcast([P, P]), ident[:])
+        rw_all = psum.tile([P, 2, HALF], F32, name="rw_all")
+        for h in range(2):
+            nc.tensor.transpose(rw_all[:, h, :], rw_col[:, h : h + 1].to_broadcast([P, P]), ident[:])
 
         pick_a = [tile("last_a%d" % h, [P, HALF], F32) for h in range(2)]
         pick_b = [tile("last_b%d" % h, [P, HALF], F32) for h in range(2)]
+        larger = [tile("last_larger%d" % h, [P, HALF], F32) for h in range(2)]
         gather(True, pick_a[0][:], x_planes[last][:], list_a[:, half_list(0)])
         gather(False, pick_b[0][:], x_planes[last][:], list_b[:, half_list(0)])
         gather(False, pick_a[1][:], x_planes[last][:], list_a[:, half_list(1)])
@@ -179,22 +199,23 @@ def tile_list_largerpicks_plain_floored_pl_kernel(
         u1_scales = [tile("u1_scales%d" % h, [P, HALF], U8) for h in range(2)]
 
         def last_max(h):
-            nc.vector.tensor_tensor(
-                out=larger[1][:, PACK - 1, half_cols(h)], in0=pick_a[h][:], in1=pick_b[h][:], op=MAX
-            )
+            nc.vector.tensor_tensor(out=larger[h][:], in0=pick_a[h][:], in1=pick_b[h][:], op=MAX)
+
+        def last_scale(h):
+            scale(h == 0, u_planes[:, PACK - 1, half_cols(h)], larger[h][:], last)
 
         last_max(0)
-        w_dealt = [tile("w_dealt0", [P, R], U32, tag="last_a0")]
-        deal(w_dealt[0][:], w_raw[0][:], 4)
-        scale_and_round(u1[0][:], larger[1][:, :, half_cols(0)], 1)
-        w_dealt.append(tile("w_dealt1", [P, R], U32, tag="w_raw0"))
+        last_scale(0)
+        last_max(1)
+        interleave(nc.vector.tensor_copy, u1[0][:], u_planes[:, :, half_cols(0)])
+        last_scale(1)
+        interleave(nc.scalar.copy, u1[1][:], u_planes[:, :, half_cols(1)])
+        w_dealt.append(tile("w_dealt1", [P, R], U32, tag="last_larger0"))
         deal(w_dealt[1][:], w_raw[1][:], 4)
         quantize(u1_codes[0][:], u1_scales[0][:], u1[0][:], E5M2)
-        last_max(1)
-        scale_and_round(u1[1][:], larger[1][:, :, half_cols(1)], 1)
-        quantize(u1_codes[1][:], u1_scales[1][:], u1[1][:], E5M2)
-        wb_dealt = tile("wb_dealt", [P, 2 * N], U8, tag="u1_1")
+        wb_dealt = tile("wb_dealt", [P, 2 * N], U8, tag="u1_0")
         deal(wb_dealt[:].bitcast(U16), wb_raw[:].bitcast(U16), 8)
+        quantize(u1_codes[1][:], u1_scales[1][:], u1[1][:], E5M2)
 
         a_bank = [psum.tile([P, PACK, HALF], F32, name="a_bank%d" % h) for h in range(2)]
 
@@ -215,12 +236,6 @@ def tile_list_largerpicks_plain_floored_pl_kernel(
         first_product(0, 1, u1_codes[0][:], u1_scales[0][:])
         first_product(1, 1, u1_codes[1][:], u1_scales[1][:])
 
-        def gather_floor(on_vector, h):
-            high = tile("floor_high%d" % h, [P, 2, HALF], F32, tag="hid%d" % h)
-            for t in range(2):
-                gather(on_vector, high[:, t, :], tz_planes[2 + t][:], list_z[:, half_list(h)])
-            return high
-
         hid = [tile("hid%d" % h, [P, HALF, PACK], BF16) for h in range(2)]
         hid_codes = [tile("hid_codes%d" % h, [P, HALF], U32) for h in range(2)]
         hid_scales = [tile("hid_scales%d" % h, [P, HALF], U8) for h in range(2)]
@@ -240,13 +255,16 @@ def tile_list_largerpicks_plain_floored_pl_kernel(
                     stop=True,
                 )
 
-        floor_low = tile("floor_low", [P, 2, J], F32, tag="x%d" % last)
-        for t in range(2):
-            gather(False, floor_low[:, t, :], tz_planes[t][:], list_z[:])
+        def gather_floor(h, tag, vector_planes):
+            picked = tile("floor%d" % h, [P, PACK, HALF], F32, tag=tag)
+            for t in range(PACK):
+                gather(t in vector_planes, picked[:, t, :], tz_planes[t][:], list_z[:, half_list(h)])
+            return picked
+
+        floor = [gather_floor(0, "u_planes", (2, 3))]
         second_product(0)
-        floor_high = [gather_floor(True, 0)]
         second_product(1)
-        floor_high.append(gather_floor(False, 1))
+        floor.append(gather_floor(1, "hid0", ()))
 
         y_rows = out_0.rearrange("(p t) j -> p t j", t=PACK)
         y_words = out_1[0].rearrange("p c r -> p (c r)")
@@ -257,17 +275,13 @@ def tile_list_largerpicks_plain_floored_pl_kernel(
         y_codes = [tile("y_codes%d" % h, [P, HALF], U32) for h in range(2)]
 
         def finish(h):
-            low = floor_low[:, :, half_cols(h)]
-            high = floor_high[h][:]
-            nc.vector.tensor_tensor(out=floored[h][:, 0:2, :], in0=p_bank[h][:, 0:2, :], in1=low, op=MAX)
-            nc.vector.tensor_tensor(out=floored[h][:, 2:4, :], in0=p_bank[h][:, 2:4, :], in1=high, op=MAX)
-            weights = rw_all[:, :, h * (P // 2) : (h + 1) * (P // 2)].rearrange("p e q -> p q e")
-            nc.vector.tensor_tensor(
-                out=y[h][:].rearrange("p t (q e) -> p t q e", e=2),
-                in0=floored[h][:].rearrange("p t (q e) -> p t q e", e=2),
-                in1=weights.unsqueeze(1).to_broadcast([P, PACK, P // 2, 2]),
-                op=MULT,
-            )
+            weights = rw_all[:, h : h + 1, :].to_broadcast([P, 2, HALF])
+            for s in range(2):
+                pair = slice(2 * s, 2 * s + 2)
+                nc.vector.tensor_tensor(out=floored[h][:, pair, :], in0=p_bank[h][:, pair, :], in1=floor[h][:, pair, :], op=MAX)
+            for s in range(2):
+                pair = slice(2 * s, 2 * s + 2)
+                nc.vector.tensor_tensor(out=y[h][:, pair, :], in0=floored[h][:, pair, :], in1=weights, op=MULT)
             nc.sync.dma_start(out=y_rows[:, :, half_cols(h)], in_=y[h][:])
 
         def planes(h):
@@ -277,10 +291,10 @@ def tile_list_largerpicks_plain_floored_pl_kernel(
             )
 
         finish(0)
-        nc.scalar.copy(out=y_grouped[0][:], in_=y[0][:].rearrange("p t j -> p j t"))
+        interleave(nc.scalar.copy, y_grouped[0][:], y[0][:])
         finish(1)
+        interleave(nc.vector.tensor_copy, y_grouped[1][:], y[1][:])
         planes(0)
-        nc.vector.tensor_copy(out=y_grouped[1][:], in_=y[1][:].rearrange("p t j -> p j t"))
         planes(1)
         for q in range(4):
             queue = nc.sync if q % 2 == 0 else nc.scalar

from contextlib import ExitStack

import concourse.mybir as mybir
from concourse.masks import make_identity

K, T, J, R, N, Z = 1024, 1024, 256, 512, 512, 512
FLOPS = 2 * K * R * J + 2 * R * N * J

F32 = mybir.dt.float32
BF16 = mybir.dt.bfloat16
I32 = mybir.dt.int32
U32 = mybir.dt.uint32
U16 = mybir.dt.uint16
U8 = mybir.dt.uint8
E5M2 = mybir.dt.float8_e5m2_x4
E4M3 = mybir.dt.float8_e4m3fn_x4
E2M1 = mybir.dt.float4_e2m1fn_x4
MAX = mybir.AluOpType.max
MULT = mybir.AluOpType.mult
COPY = mybir.ActivationFunctionType.Copy
RELU = mybir.ActivationFunctionType.Relu

P = 128
PACK = 4
PASSES = K // (P * PACK)
HALF = J // 2
LIST_COLS = J // 16


def tile_list_largerpicks_plain_floored_pl_kernel(
    tc, xf, fk, w_words, w_scales, wb_words, wb_scales, tz, rw, offs, offs2, offs3, out_0, out_1, out_2
):
    nc = tc.nc
    with ExitStack() as ctx:
        keep = ctx.enter_context(tc.tile_pool(name="keep", bufs=1))
        psum = ctx.enter_context(tc.psum_pool(name="psum", bufs=1))

        def tile(name, shape, dtype, tag=""):
            return keep.tile(shape, dtype, name=name, tag=tag or name, align_bytes=64)

        list_a = tile("list_a", [P, LIST_COLS], U16)
        list_b = tile("list_b", [P, LIST_COLS], U16)
        list_z = tile("list_z", [P, LIST_COLS], U16)
        x_planes = [tile("x%d" % i, [P, T], F32) for i in range(PASSES * PACK)]
        tz_planes = [tile("tz%d" % t, [P, Z], F32) for t in range(PACK)]
        fk_sb = tile("fk_sb", [P, PASSES, PACK], F32)
        rw_col = tile("rw_col", [P, 2], F32)
        ident = tile("ident", [P, P], F32)
        w_raw = [tile("w_raw%d" % g, [P, R], U32) for g in range(PASSES)]
        ws_raw = tile("ws_raw", [P, PASSES, R], U8)
        ws_dealt = tile("ws_dealt", [P, PASSES, R], U8)
        wb_raw = tile("wb_raw", [P, 2 * N], U8)
        wbs_raw = tile("wbs_raw", [P, N], U8)

        x_rows = xf.rearrange("(g p t) c -> g t p c", p=P, t=PACK)
        tz_rows = tz.rearrange("(p t) z -> t p z", t=PACK)

        zero_col = tile("zero_col", [P, 1], F32)
        nc.vector.memset(zero_col[:], 0.0)
        nc.scalar.activation(ident[:], zero_col[:].to_broadcast([P, P]), COPY)
        nc.gpsimd.memset(ws_raw[:].rearrange("p g c -> p (g c)").bitcast(U32), 0)
        nc.gpsimd.memset(wbs_raw[:].bitcast(U32), 0)
        make_identity(nc, ident[:], nomemset=True)

        def load_x(i):
            nc.sync.dma_start(out=x_planes[i][:], in_=x_rows[i // PACK, i % PACK])

        def load_w(g):
            nc.sync.dma_start(
                out=w_raw[g][:].bitcast(I32), in_=w_words[g].rearrange("p c r -> p (c r)").bitcast(I32)
            )

        def load_w_scales(q):
            nc.sync.dma_start(
                out=ws_raw[32 * q : 32 * q + 4, :, :].bitcast(I32),
                in_=w_scales[:, 4 * q : 4 * q + 4, :].rearrange("g r c -> r g c").bitcast(I32),
            )

        def load_wb_scales(q):
            nc.gpsimd.dma_start(
                out=wbs_raw[32 * q : 32 * q + 4, :].bitcast(I32),
                in_=wb_scales[0, 4 * q : 4 * q + 4, :].bitcast(I32),
            )

        for q in range(4):
            load_wb_scales(q)
        load_x(0)
        nc.sync.dma_start(list_a[:], offs)
        nc.sync.dma_start(list_b[:], offs2)
        load_x(1)
        nc.sync.dma_start(out=fk_sb[:], in_=fk.rearrange("(g p t) o -> p g (t o)", p=P, t=PACK))
        load_x(2)
        load_w_scales(0)
        load_w_scales(1)
        load_x(3)
        load_w_scales(2)
        load_w_scales(3)
        load_x(4)
        load_x(5)
        with nc.allow_non_contiguous_dma(reason="one weight to a partition"):
            nc.sync.dma_start(out=rw_col[:], in_=rw.rearrange("o (h p) -> p (o h)", p=P))
        load_w(0)
        load_x(6)
        load_x(7)
        load_w(1)
        nc.sync.dma_start(out=wb_raw[:].bitcast(I32), in_=wb_words[0].bitcast(I32))
        nc.sync.dma_start(list_z[:], offs3)
        for t in range(PACK):
            nc.sync.dma_start(out=tz_planes[t][:], in_=tz_rows[t])

        def gather(on_vector, out, window, offsets):
            if on_vector:
                nc.vector.tensor_copy(out, window.indirect(offsets))
            else:
                nc.scalar.activation(out, window.indirect(offsets), COPY)

        def deal(out, in_, run):
            nc.vector.tensor_copy(
                out=out.rearrange("p (t c i) -> p c t i", t=PACK, i=run),
                in_=in_.rearrange("p (c i t) -> p c t i", t=PACK, i=run),
            )

        def half_cols(h):
            return slice(h * HALF, (h + 1) * HALF)

        def half_list(h):
            return slice(h * LIST_COLS // 2, (h + 1) * LIST_COLS // 2)

        def interleave(copy, out, in_):
            copy(
                out=out.rearrange("p (c i) t -> p c t i", i=4),
                in_=in_.rearrange("p t (c i) -> p c t i", i=4),
            )

        def quantize(codes, scales, grouped, fmt):
            nc.vector.quantize_mx(
                out=codes.bitcast(fmt), scales=scales, in_=grouped.rearrange("p j t -> p (j t)")
            )

        u_planes = tile("u_planes", [P, PACK, J], BF16)
        larger0 = tile("larger0", [P, PACK, J], F32)
        vector_gathers = (0, 1, 2)
        last = PASSES * PACK - 1

        def scale(on_vector, out, larger, i):
            factor = fk_sb[:, i // PACK, i % PACK : i % PACK + 1]
            if on_vector:
                nc.vector.tensor_scalar(out, larger, factor, None, MULT)
            else:
                nc.scalar.activation(out, larger, COPY, scale=factor)

        def plane(i):
            pick_a = tile("pick_a%d" % i, [P, J], F32)
            pick_b = tile("pick_b%d" % i, [P, J], F32)
            larger = larger0[:, i, :] if i < PACK else tile("larger%d" % i, [P, J], F32)[:]
            gather(i in vector_gathers, pick_a[:], x_planes[i][:], list_a[:])
            gather(False, pick_b[:], x_planes[i][:], list_b[:])
            nc.vector.tensor_tensor(out=larger, in0=pick_a[:], in1=pick_b[:], op=MAX)
            if i >= PACK:
                scale(True, u_planes[:, i % PACK, :], larger, i)

        u0 = tile("u0", [P, J, PACK], BF16)
        u0_codes = tile("u0_codes", [P, J], U32)
        u0_scales = tile("u0_scales", [P, J], U8)
        for i in range(PACK - 1):
            plane(i)
        for g in range(PASSES):
            deal(ws_dealt[:, g, :], ws_raw[:, g, :], 16)
        plane(PACK - 1)
        nc.vector.tensor_tensor(
            out=u0[:],
            in0=larger0[:].rearrange("p t j -> p j t"),
            in1=fk_sb[:, 0:1, :].to_broadcast([P, J, PACK]),
            op=MULT,
        )
        plane(PACK)
        quantize(u0_codes[:], u0_scales[:], u0[:], E5M2)
        w_dealt = [tile("w_dealt0", [P, R], U32, tag="pick_a%d" % PACK)]
        deal(w_dealt[0][:], w_raw[0][:], 4)
        plane(PACK + 1)
        wbs_dealt = tile("wbs_dealt", [P, N], U8, tag="pick_a%d" % (PACK + 1))
        deal(wbs_dealt[:], wbs_raw[:], 16)
        plane(PACK + 2)

        rw_all = psum.tile([P, 2, HALF], F32, name="rw_all")
        for h in range(2):
            nc.tensor.transpose(rw_all[:, h, :], rw_col[:, h : h + 1].to_broadcast([P, P]), ident[:])

        pick_a = [tile("last_a%d" % h, [P, HALF], F32) for h in range(2)]
        pick_b = [tile("last_b%d" % h, [P, HALF], F32) for h in range(2)]
        larger = [tile("last_larger%d" % h, [P, HALF], F32) for h in range(2)]
        gather(True, pick_a[0][:], x_planes[last][:], list_a[:, half_list(0)])
        gather(False, pick_b[0][:], x_planes[last][:], list_b[:, half_list(0)])
        gather(False, pick_a[1][:], x_planes[last][:], list_a[:, half_list(1)])
        gather(False, pick_b[1][:], x_planes[last][:], list_b[:, half_list(1)])

        u1 = [tile("u1_%d" % h, [P, HALF, PACK], BF16) for h in range(2)]
        u1_codes = [tile("u1_codes%d" % h, [P, HALF], U32) for h in range(2)]
        u1_scales = [tile("u1_scales%d" % h, [P, HALF], U8) for h in range(2)]

        def last_max(h):
            nc.vector.tensor_tensor(out=larger[h][:], in0=pick_a[h][:], in1=pick_b[h][:], op=MAX)

        def last_scale(h):
            scale(h == 0, u_planes[:, PACK - 1, half_cols(h)], larger[h][:], last)

        last_max(0)
        last_scale(0)
        last_max(1)
        interleave(nc.vector.tensor_copy, u1[0][:], u_planes[:, :, half_cols(0)])
        last_scale(1)
        interleave(nc.scalar.copy, u1[1][:], u_planes[:, :, half_cols(1)])
        w_dealt.append(tile("w_dealt1", [P, R], U32, tag="last_larger0"))
        deal(w_dealt[1][:], w_raw[1][:], 4)
        quantize(u1_codes[0][:], u1_scales[0][:], u1[0][:], E5M2)
        wb_dealt = tile("wb_dealt", [P, 2 * N], U8, tag="u1_0")
        deal(wb_dealt[:].bitcast(U16), wb_raw[:].bitcast(U16), 8)
        quantize(u1_codes[1][:], u1_scales[1][:], u1[1][:], E5M2)

        a_bank = [psum.tile([P, PACK, HALF], F32, name="a_bank%d" % h) for h in range(2)]

        def first_product(h, g, codes, scales):
            for t in range(PACK):
                nc.tensor.matmul_mx(
                    out=a_bank[h][:, t, :],
                    lhsT=w_dealt[g][:, t * P : (t + 1) * P].bitcast(E5M2),
                    lhsT_scale=ws_dealt[:, g, t * P : (t + 1) * P],
                    rhs=codes.bitcast(E5M2),
                    rhs_scale=scales,
                    start=(g == 0 and t == 0),
                    stop=(g == PASSES - 1 and t == PACK - 1),
                )

        first_product(0, 0, u0_codes[:, half_cols(0)], u0_scales[:, half_cols(0)])
        first_product(1, 0, u0_codes[:, half_cols(1)], u0_scales[:, half_cols(1)])
        first_product(0, 1, u1_codes[0][:], u1_scales[0][:])
        first_product(1, 1, u1_codes[1][:], u1_scales[1][:])

        hid = [tile("hid%d" % h, [P, HALF, PACK], BF16) for h in range(2)]
        hid_codes = [tile("hid_codes%d" % h, [P, HALF], U32) for h in range(2)]
        hid_scales = [tile("hid_scales%d" % h, [P, HALF], U8) for h in range(2)]
        p_bank = [psum.tile([P, PACK, HALF], F32, name="p_bank%d" % h) for h in range(2)]

        def second_product(h):
            nc.scalar.activation(hid[h][:], a_bank[h][:].rearrange("p t j -> p j t"), RELU)
            quantize(hid_codes[h][:], hid_scales[h][:], hid[h][:], E5M2)
            for t in range(PACK):
                nc.tensor.matmul_mx(
                    out=p_bank[h][:, t, :],
                    lhsT=wb_dealt[:, 2 * t * P : 2 * (t + 1) * P].bitcast(E2M1),
                    lhsT_scale=wbs_dealt[:, t * P : (t + 1) * P],
                    rhs=hid_codes[h][:].bitcast(E5M2),
                    rhs_scale=hid_scales[h][:],
                    start=True,
                    stop=True,
                )

        def gather_floor(h, tag, vector_planes):
            picked = tile("floor%d" % h, [P, PACK, HALF], F32, tag=tag)
            for t in range(PACK):
                gather(t in vector_planes, picked[:, t, :], tz_planes[t][:], list_z[:, half_list(h)])
            return picked

        floor = [gather_floor(0, "u_planes", (2, 3))]
        second_product(0)
        second_product(1)
        floor.append(gather_floor(1, "hid0", ()))

        y_rows = out_0.rearrange("(p t) j -> p t j", t=PACK)
        y_words = out_1[0].rearrange("p c r -> p (c r)")
        y_scales = tile("y_scales", [P, J], U8)
        floored = [tile("floored%d" % h, [P, PACK, HALF], F32) for h in range(2)]
        y = [tile("y%d" % h, [P, PACK, HALF], F32) for h in range(2)]
        y_grouped = [tile("y_grouped%d" % h, [P, HALF, PACK], BF16) for h in range(2)]
        y_codes = [tile("y_codes%d" % h, [P, HALF], U32) for h in range(2)]

        def finish(h):
            weights = rw_all[:, h : h + 1, :].to_broadcast([P, 2, HALF])
            for s in range(2):
                pair = slice(2 * s, 2 * s + 2)
                nc.vector.tensor_tensor(out=floored[h][:, pair, :], in0=p_bank[h][:, pair, :], in1=floor[h][:, pair, :], op=MAX)
            for s in range(2):
                pair = slice(2 * s, 2 * s + 2)
                nc.vector.tensor_tensor(out=y[h][:, pair, :], in0=floored[h][:, pair, :], in1=weights, op=MULT)
            nc.sync.dma_start(out=y_rows[:, :, half_cols(h)], in_=y[h][:])

        def planes(h):
            quantize(y_codes[h][:], y_scales[:, half_cols(h)], y_grouped[h][:], E4M3)
            nc.sync.dma_start(
                out=y_words[:, PACK * h * HALF : PACK * (h + 1) * HALF].bitcast(I32), in_=y_codes[h][:].bitcast(I32)
            )

        finish(0)
        interleave(nc.scalar.copy, y_grouped[0][:], y[0][:])
        finish(1)
        interleave(nc.vector.tensor_copy, y_grouped[1][:], y[1][:])
        planes(0)
        planes(1)
        for q in range(4):
            queue = nc.sync if q % 2 == 0 else nc.scalar
            queue.dma_start(
                out=out_2[0, 4 * q : 4 * q + 4, :].bitcast(I32), in_=y_scales[32 * q : 32 * q + 4, :].bitcast(I32)
            )
